import numpy as np
import ml_dtypes


def mxq(x, axis, fmt="e4m3"):
    dtype, down = {"e4m3": (ml_dtypes.float8_e4m3fn, 7), "e5m2": (ml_dtypes.float8_e5m2, 14)}[fmt]
    v = np.moveaxis(np.asarray(x, np.float32).astype(ml_dtypes.bfloat16).astype(np.float64), axis, -1)
    blocks = v.reshape(v.shape[:-1] + (-1, 32))
    amax = np.abs(blocks).max(-1, keepdims=True)
    byte = np.maximum(np.where(amax > 0, np.frexp(amax)[1] - 1 + 127, 0) - down, 1)
    scale = np.exp2(byte - 127.0)
    codes = (blocks / scale).astype(np.float32).astype(dtype).astype(np.float64)
    return np.moveaxis((codes * scale).reshape(v.shape), -1, axis)


WIDE = False


def mx_kscale(k):
    if not WIDE:
        return np.ones(k)
    levels = np.array([10, -10, 5, -5, 0])
    if k % 512:
        return np.exp2(np.random.permutation(np.resize(levels, k // 32))).repeat(32)
    a = np.empty((k // 512, 16))
    for p in range(k // 512):
        a[p, :8] = np.random.permutation(np.resize(levels, 8))
        for g in range(8):
            far = levels[np.abs(levels - a[p, g]) >= 10]
            a[p, g + 8] = far[np.random.randint(len(far))]
    return np.exp2(a.ravel()).repeat(32)


def f64(x):
    return np.asarray(x).astype(np.float64)


E2M1 = np.array([0.0, 0.5, 1.0, 1.5, 2.0, 3.0, 4.0, 6.0, -0.0, -0.5, -1.0, -1.5, -2.0, -3.0, -4.0, -6.0])


def pack_weight(w, fmt):
    k, n = w.shape
    w = f64(np.asarray(w, np.float32).astype(ml_dtypes.bfloat16)).reshape(k // 32, 32, n)
    amax = np.abs(w).max(1)
    if fmt == "e4m3":
        byte = np.frexp(amax)[1] - 1 + 127 - 7
    else:
        mant, ex = np.frexp(amax / 6.0)
        byte = np.where(mant > 0.5, ex, ex - 1) + 127
    byte = np.clip(np.where(amax > 0, byte, 1), 1, 254)
    scaled = (w * np.exp2(127.0 - byte)[:, None, :]).reshape(k, n).astype(np.float32)
    by_word = np.ascontiguousarray(scaled.reshape(k // 512, 128, 4, n).transpose(0, 1, 3, 2))
    if fmt == "e4m3":
        words = by_word.astype(ml_dtypes.float8_e4m3fn).view(np.uint8)
    else:
        c = by_word.astype(ml_dtypes.float4_e2m1fn).view(np.uint8) & 0xF
        words = (c[..., 0::2] | (c[..., 1::2] << 4)).reshape(k // 512, 128, 2 * n)
    return np.ascontiguousarray(words), np.ascontiguousarray(byte.astype(np.uint8).reshape(k // 512, 16, n))


def unpack_weight(words, scales, fmt):
    g, _, n = scales.shape
    words = np.ascontiguousarray(words).reshape(g, 128, n, -1)
    if fmt == "e4m3":
        vals = words.view(ml_dtypes.float8_e4m3fn).astype(np.float64)
    else:
        nib = np.empty((g, 128, n, 4), np.uint8)
        nib[..., 0::2] = words & 0xF
        nib[..., 1::2] = words >> 4
        vals = E2M1[nib]
    vals = vals * np.repeat(np.exp2(scales.astype(np.float64) - 127.0), 8, axis=1)[..., None]
    return vals.transpose(0, 1, 3, 2).reshape(g * 512, n)


def silu(v):
    return v / (1.0 + np.exp(-np.maximum(v, -700.0)))


K, M, T = 2048, 512, 1024


def setup_inputs():
    n = np.random.standard_normal
    s = mx_kscale(K)[:, None]
    p_w4 = pack_weight(n((K, M)) / np.sqrt(K) / s, "e2m1")
    p_w8 = pack_weight(n((K, M)) / np.sqrt(K) / s, "e4m3")
    return {
        "x": (n((K, T)) * s).astype(np.float32),
        "w4_words": p_w4[0],
        "w4_scales": p_w4[1],
        "w8_words": p_w8[0],
        "w8_scales": p_w8[1],
    }


def reference(x, w4_words, w4_scales, w8_words, w8_scales):
    x_ = mxq(f64(x), 0, "e4m3")
    w4_ = unpack_weight(w4_words, w4_scales, "e2m1")
    w8_ = unpack_weight(w8_words, w8_scales, "e4m3")
    y = w4_.T @ x_
    u = w8_.T @ x_
    y = silu(y) * u
    return y

@@ -1,0 +1,171 @@
+from contextlib import ExitStack
+
+import concourse.mybir as mybir
+
+K, M, T = 2048, 512, 1024
+FLOPS = 2 * 2 * K * M * T
+
+F32 = mybir.dt.float32
+BF16 = mybir.dt.bfloat16
+I32 = mybir.dt.int32
+U32 = mybir.dt.uint32
+U8 = mybir.dt.uint8
+FP8X4 = mybir.dt.float8_e4m3fn_x4
+FP4X4 = mybir.dt.float4_e2m1fn_x4
+ACT = mybir.ActivationFunctionType
+ALU = mybir.AluOpType
+
+P = 128
+PASSES = K // 512
+HALF = 512
+M_TILES = M // 128
+V_COLS = 352
+
+
+def tile_mix_glu48_fm_none_kernel(tc, x, w4_words, w4_scales, w8_words, w8_scales, out):
+    nc = tc.nc
+    with ExitStack() as ctx:
+        keep = ctx.enter_context(tc.tile_pool(name="keep", bufs=1))
+        psum = ctx.enter_context(tc.psum_pool(name="psum", bufs=1))
+        ctx.enter_context(tc.manual_schedule())
+
+        sc4 = keep.tile([P, PASSES * M], U8, align_bytes=64, name="sc4")
+        sc8 = keep.tile([P, M], U8, align_bytes=64, name="sc8")
+        dummy = keep.tile([P, 8], F32, align_bytes=64, name="dummy")
+        nc.vector.memset(sc8[:].bitcast(I32), 0)
+        nc.vector.memset(sc4[:].bitcast(I32), 0)
+        nc.vector.memset(dummy[:], 0.0)
+        nc.scalar.activation(out=dummy[:, 0:1], in_=dummy[:, 1:2], func=ACT.Silu)
+
+        raw = {}
+        w4 = {}
+        w8 = {}
+
+        def load_x(h, a):
+            raw[h, a] = keep.tile([P, 4, HALF], F32, align_bytes=64, name="raw_%d_%d" % (h, a))
+            nc.sync.dma_start(
+                out=raw[h, a][:],
+                in_=x[512 * a : 512 * (a + 1), HALF * h : HALF * (h + 1)].rearrange("(p j) w -> p j w", j=4),
+            )
+
+        def load_w(a):
+            w8[a] = keep.tile([P, 4 * M], U8, align_bytes=64, name="w8_%d" % a)
+            w4[a] = keep.tile([P, 2 * M], U8, align_bytes=64, name="w4_%d" % a)
+            nc.sync.dma_start(out=w4[a][:].bitcast(I32), in_=w4_words[a].bitcast(I32))
+            nc.sync.dma_start(out=w8[a][:].bitcast(I32), in_=w8_words[a].rearrange("p n i -> p (n i)").bitcast(I32))
+
+        def load_scales():
+            for q in range(4):
+                nc.scalar.dma_start(
+                    out=sc8[32 * q : 32 * q + 16, :].bitcast(I32),
+                    in_=w8_scales[:, 4 * q : 4 * q + 4, :].bitcast(I32),
+                )
+            for q in range(4):
+                nc.scalar.dma_start(
+                    out=sc4[32 * q : 32 * q + 4, :].bitcast(I32).rearrange("r (a n) -> r a n", a=PASSES),
+                    in_=w4_scales[:, 4 * q : 4 * q + 4, :].bitcast(I32).rearrange("a r n -> r a n"),
+                )
+
+        load_x(0, 0)
+        load_scales()
+        load_w(0)
+        for a in range(1, PASSES):
+            load_x(0, a)
+            load_w(a)
+        for a in range(PASSES):
+            load_x(1, a)
+
+        grouped = {}
+        codes = {}
+        scales = {}
+
+        def interleave(engine_copy, h, a, lo, hi):
+            engine_copy(
+                out=grouped[h, a][:, lo:hi, :].rearrange("p (c i) t -> p c t i", i=4),
+                in_=raw[h, a][:, :, lo:hi].rearrange("p t (c i) -> p c t i", i=4),
+            )
+
+        def copy_v(h, a):
+            grouped[h, a] = keep.tile([P, HALF, 4], BF16, align_bytes=64, name="grouped_%d_%d" % (h, a))
+            codes[h, a] = keep.tile([P, HALF], U32, align_bytes=64, name="codes_%d_%d" % (h, a))
+            scales[h, a] = keep.tile([P, HALF], U8, align_bytes=64, name="scales_%d_%d" % (h, a))
+            interleave(nc.vector.tensor_copy, h, a, 0, 256)
+            interleave(nc.vector.tensor_copy, h, a, 256, V_COLS)
+
+        def copy_s(h, a):
+            interleave(nc.scalar.copy, h, a, V_COLS, HALF)
+
+        def quantize(h, a):
+            for lo in (0, 256):
+                nc.vector.quantize_mx(
+                    out=codes[h, a][:, lo : lo + 256].bitcast(FP8X4),
+                    scales=scales[h, a][:, lo : lo + 256],
+                    in_=grouped[h, a][:, lo : lo + 256, :].rearrange("p w t -> p (w t)"),
+                )
+
+        g = {}
+        u = {}
+
+        def multiply(h, a):
+            for m in range(M_TILES):
+                if a == 0:
+                    g[h, m] = psum.tile([P, HALF], F32, name="g_%d_%d" % (h, m), tag="g_%d" % m)
+                    u[h, m] = psum.tile([P, HALF], F32, name="u_%d_%d" % (h, m), tag="u_%d" % m)
+                cols = slice(128 * m, 128 * (m + 1))
+                nc.tensor.matmul_mx(
+                    out=g[h, m][:],
+                    lhsT=w4[a][:, 256 * m : 256 * (m + 1)].bitcast(FP4X4),
+                    lhsT_scale=sc4[:, M * a + 128 * m : M * a + 128 * (m + 1)],
+                    rhs=codes[h, a][:].bitcast(FP8X4),
+                    rhs_scale=scales[h, a][:],
+                    start=(a == 0),
+                    stop=(a == PASSES - 1),
+                )
+                nc.tensor.matmul_mx(
+                    out=u[h, m][:],
+                    lhsT=w8[a][:, 512 * m : 512 * (m + 1)].bitcast(FP8X4),
+                    lhsT_scale=sc8[4 * a : P, cols],
+                    rhs=codes[h, a][:].bitcast(FP8X4),
+                    rhs_scale=scales[h, a][:],
+                    start=(a == 0),
+                    stop=(a == PASSES - 1),
+                )
+
+        gate = {}
+        res = {}
+
+        def silu(h, m):
+            gate[h, m] = keep.tile([P, HALF], F32, align_bytes=64, name="gate_%d_%d" % (h, m))
+            nc.scalar.activation(out=gate[h, m][:], in_=g[h, m][:], func=ACT.Silu)
+
+        def mul(h, m):
+            res[h, m] = keep.tile([P, HALF], F32, align_bytes=64, name="res_%d_%d" % (h, m))
+            nc.vector.tensor_tensor(out=res[h, m][:], in0=u[h, m][:], in1=gate[h, m][:], op=ALU.mult)
+            nc.sync.dma_start(
+                out=out[128 * m : 128 * (m + 1), HALF * h : HALF * (h + 1)], in_=res[h, m][:]
+            )
+
+        for a in range(PASSES):
+            copy_v(0, a)
+            copy_s(0, a)
+            quantize(0, a)
+            multiply(0, a)
+        silu(0, 0)
+        silu(0, 1)
+        copy_v(1, 0)
+        copy_s(1, 0)
+        mul(0, 0)
+        quantize(1, 0)
+        silu(0, 2)
+        silu(0, 3)
+        for m in (1, 2, 3):
+            mul(0, m)
+        multiply(1, 0)
+        for a in range(1, PASSES):
+            copy_v(1, a)
+            copy_s(1, a)
+            quantize(1, a)
+            multiply(1, a)
+        for m in range(M_TILES):
+            silu(1, m)
+            mul(1, m)

@@ -33,7 +33,7 @@ def tile_mix_glu48_fm_none_kernel(tc, x, w4_words, w4_scales, w8_words, w8_scale
         sc8 = keep.tile([P, M], U8, align_bytes=64, name="sc8")
         dummy = keep.tile([P, 8], F32, align_bytes=64, name="dummy")
         nc.vector.memset(sc8[:].bitcast(I32), 0)
-        nc.vector.memset(sc4[:].bitcast(I32), 0)
+        nc.gpsimd.memset(sc4[:].bitcast(I32), 0)
         nc.vector.memset(dummy[:], 0.0)
         nc.scalar.activation(out=dummy[:, 0:1], in_=dummy[:, 1:2], func=ACT.Silu)
 
@@ -41,18 +41,24 @@ def tile_mix_glu48_fm_none_kernel(tc, x, w4_words, w4_scales, w8_words, w8_scale
         w4 = {}
         w8 = {}
 
-        def load_x(h, a):
-            raw[h, a] = keep.tile([P, 4, HALF], F32, align_bytes=64, name="raw_%d_%d" % (h, a))
-            nc.sync.dma_start(
-                out=raw[h, a][:],
-                in_=x[512 * a : 512 * (a + 1), HALF * h : HALF * (h + 1)].rearrange("(p j) w -> p j w", j=4),
-            )
+        def load_x(h, a, pieces=1):
+            width = HALF // pieces
+            for c in range(pieces):
+                t = keep.tile([P, 4, width], F32, align_bytes=64, name="raw_%d_%d_%d" % (h, a, c))
+                for lo in range(0, width, 256):
+                    raw[h, a, width * c + lo] = t[:, :, lo : lo + 256]
+                nc.sync.dma_start(
+                    out=t[:],
+                    in_=x[512 * a : 512 * (a + 1), HALF * h + width * c : HALF * h + width * (c + 1)].rearrange(
+                        "(p j) w -> p j w", j=4
+                    ),
+                )
 
         def load_w(a):
             w8[a] = keep.tile([P, 4 * M], U8, align_bytes=64, name="w8_%d" % a)
             w4[a] = keep.tile([P, 2 * M], U8, align_bytes=64, name="w4_%d" % a)
-            nc.sync.dma_start(out=w4[a][:].bitcast(I32), in_=w4_words[a].bitcast(I32))
             nc.sync.dma_start(out=w8[a][:].bitcast(I32), in_=w8_words[a].rearrange("p n i -> p (n i)").bitcast(I32))
+            nc.sync.dma_start(out=w4[a][:].bitcast(I32), in_=w4_words[a].bitcast(I32))
 
         def load_scales():
             for q in range(4):
@@ -61,111 +67,149 @@ def tile_mix_glu48_fm_none_kernel(tc, x, w4_words, w4_scales, w8_words, w8_scale
                     in_=w8_scales[:, 4 * q : 4 * q + 4, :].bitcast(I32),
                 )
             for q in range(4):
-                nc.scalar.dma_start(
+                nc.gpsimd.dma_start(
                     out=sc4[32 * q : 32 * q + 4, :].bitcast(I32).rearrange("r (a n) -> r a n", a=PASSES),
                     in_=w4_scales[:, 4 * q : 4 * q + 4, :].bitcast(I32).rearrange("a r n -> r a n"),
                 )
 
-        load_x(0, 0)
         load_scales()
+        load_x(0, 0, 2)
         load_w(0)
         for a in range(1, PASSES):
             load_x(0, a)
             load_w(a)
-        for a in range(PASSES):
+        for a in range(PASSES - 1):
             load_x(1, a)
+        load_x(1, PASSES - 1, 2)
 
         grouped = {}
         codes = {}
         scales = {}
 
         def interleave(engine_copy, h, a, lo, hi):
+            base = lo // 256 * 256
             engine_copy(
                 out=grouped[h, a][:, lo:hi, :].rearrange("p (c i) t -> p c t i", i=4),
-                in_=raw[h, a][:, :, lo:hi].rearrange("p t (c i) -> p c t i", i=4),
+                in_=raw[h, a, base][:, :, lo - base : hi - base].rearrange("p t (c i) -> p c t i", i=4),
             )
 
-        def copy_v(h, a):
+        def tiles(h, a):
             grouped[h, a] = keep.tile([P, HALF, 4], BF16, align_bytes=64, name="grouped_%d_%d" % (h, a))
             codes[h, a] = keep.tile([P, HALF], U32, align_bytes=64, name="codes_%d_%d" % (h, a))
             scales[h, a] = keep.tile([P, HALF], U8, align_bytes=64, name="scales_%d_%d" % (h, a))
+
+        def quantize(h, a, lo):
+            nc.vector.quantize_mx(
+                out=codes[h, a][:, lo : lo + 256].bitcast(FP8X4),
+                scales=scales[h, a][:, lo : lo + 256],
+                in_=grouped[h, a][:, lo : lo + 256, :].rearrange("p w t -> p (w t)"),
+            )
+
+        def copies_whole(h, a):
+            tiles(h, a)
             interleave(nc.vector.tensor_copy, h, a, 0, 256)
             interleave(nc.vector.tensor_copy, h, a, 256, V_COLS)
-
-        def copy_s(h, a):
             interleave(nc.scalar.copy, h, a, V_COLS, HALF)
 
-        def quantize(h, a):
+        def prepare_pieces(h, a):
+            tiles(h, a)
             for lo in (0, 256):
-                nc.vector.quantize_mx(
-                    out=codes[h, a][:, lo : lo + 256].bitcast(FP8X4),
-                    scales=scales[h, a][:, lo : lo + 256],
-                    in_=grouped[h, a][:, lo : lo + 256, :].rearrange("p w t -> p (w t)"),
-                )
+                interleave(nc.vector.tensor_copy, h, a, lo, lo + 128)
+                interleave(nc.vector.tensor_copy, h, a, lo + 128, lo + 160)
+                interleave(nc.scalar.copy, h, a, lo + 160, lo + 256)
+                quantize(h, a, lo)
 
         g = {}
         u = {}
 
-        def multiply(h, a):
-            for m in range(M_TILES):
-                if a == 0:
-                    g[h, m] = psum.tile([P, HALF], F32, name="g_%d_%d" % (h, m), tag="g_%d" % m)
-                    u[h, m] = psum.tile([P, HALF], F32, name="u_%d_%d" % (h, m), tag="u_%d" % m)
-                cols = slice(128 * m, 128 * (m + 1))
-                nc.tensor.matmul_mx(
-                    out=g[h, m][:],
-                    lhsT=w4[a][:, 256 * m : 256 * (m + 1)].bitcast(FP4X4),
-                    lhsT_scale=sc4[:, M * a + 128 * m : M * a + 128 * (m + 1)],
-                    rhs=codes[h, a][:].bitcast(FP8X4),
-                    rhs_scale=scales[h, a][:],
-                    start=(a == 0),
-                    stop=(a == PASSES - 1),
-                )
-                nc.tensor.matmul_mx(
-                    out=u[h, m][:],
-                    lhsT=w8[a][:, 512 * m : 512 * (m + 1)].bitcast(FP8X4),
-                    lhsT_scale=sc8[4 * a : P, cols],
-                    rhs=codes[h, a][:].bitcast(FP8X4),
-                    rhs_scale=scales[h, a][:],
-                    start=(a == 0),
-                    stop=(a == PASSES - 1),
-                )
+        def pass_g(h, a, m, lo, hi):
+            nc.tensor.matmul_mx(
+                out=g[h, m][:, lo:hi],
+                lhsT=w4[a][:, 256 * m : 256 * (m + 1)].bitcast(FP4X4),
+                lhsT_scale=sc4[:, M * a + 128 * m : M * a + 128 * (m + 1)],
+                rhs=codes[h, a][:, lo:hi].bitcast(FP8X4),
+                rhs_scale=scales[h, a][:, lo:hi],
+                start=(a == 0),
+                stop=(a == PASSES - 1 and hi == HALF),
+            )
+
+        def pass_u(h, a, m, lo, hi):
+            nc.tensor.matmul_mx(
+                out=u[h, m][:, lo:hi],
+                lhsT=w8[a][:, 512 * m : 512 * (m + 1)].bitcast(FP8X4),
+                lhsT_scale=sc8[4 * a : P, 128 * m : 128 * (m + 1)],
+                rhs=codes[h, a][:, lo:hi].bitcast(FP8X4),
+                rhs_scale=scales[h, a][:, lo:hi],
+                start=(a == 0),
+                stop=(a == PASSES - 1 and hi == HALF),
+            )
 
         gate = {}
         res = {}
 
-        def silu(h, m):
-            gate[h, m] = keep.tile([P, HALF], F32, align_bytes=64, name="gate_%d_%d" % (h, m))
-            nc.scalar.activation(out=gate[h, m][:], in_=g[h, m][:], func=ACT.Silu)
+        def open_banks(h):
+            for m in range(M_TILES):
+                g[h, m] = psum.tile([P, HALF], F32, name="g_%d_%d" % (h, m), tag="g_%d" % m)
+                u[h, m] = psum.tile([P, HALF], F32, name="u_%d_%d" % (h, m), tag="u_%d" % m)
+                gate[h, m] = keep.tile([P, HALF], F32, align_bytes=64, name="gate_%d_%d" % (h, m))
+                res[h, m] = keep.tile([P, HALF], F32, align_bytes=64, name="res_%d_%d" % (h, m))
 
-        def mul(h, m):
-            res[h, m] = keep.tile([P, HALF], F32, align_bytes=64, name="res_%d_%d" % (h, m))
-            nc.vector.tensor_tensor(out=res[h, m][:], in0=u[h, m][:], in1=gate[h, m][:], op=ALU.mult)
+        def silu(h, m, lo=0, hi=HALF):
+            nc.scalar.activation(out=gate[h, m][:, lo:hi], in_=g[h, m][:, lo:hi], func=ACT.Silu)
+
+        def mul(h, m, lo=0, hi=HALF):
+            nc.vector.tensor_tensor(
+                out=res[h, m][:, lo:hi], in0=u[h, m][:, lo:hi], in1=gate[h, m][:, lo:hi], op=ALU.mult
+            )
+
+        def store(h, m):
             nc.sync.dma_start(
                 out=out[128 * m : 128 * (m + 1), HALF * h : HALF * (h + 1)], in_=res[h, m][:]
             )
 
-        for a in range(PASSES):
-            copy_v(0, a)
-            copy_s(0, a)
-            quantize(0, a)
+        def multiply(h, a):
+            for m in range(M_TILES):
+                pass_g(h, a, m, 0, HALF)
+                pass_u(h, a, m, 0, HALF)
+
+        open_banks(0)
+        prepare_pieces(0, 0)
+        for m in range(M_TILES):
+            pass_u(0, 0, m, 0, HALF)
+        for m in range(M_TILES):
+            pass_g(0, 0, m, 0, HALF)
+        for a in range(1, PASSES):
+            copies_whole(0, a)
+            quantize(0, a, 0)
+            quantize(0, a, 256)
             multiply(0, a)
+
+        open_banks(1)
         silu(0, 0)
         silu(0, 1)
-        copy_v(1, 0)
-        copy_s(1, 0)
+        copies_whole(1, 0)
         mul(0, 0)
-        quantize(1, 0)
+        quantize(1, 0, 0)
+        quantize(1, 0, 256)
         silu(0, 2)
         silu(0, 3)
         for m in (1, 2, 3):
             mul(0, m)
+        for m in range(M_TILES):
+            store(0, m)
         multiply(1, 0)
-        for a in range(1, PASSES):
-            copy_v(1, a)
-            copy_s(1, a)
-            quantize(1, a)
+        for a in (1, 2):
+            copies_whole(1, a)
+            quantize(1, a, 0)
+            quantize(1, a, 256)
             multiply(1, a)
+        prepare_pieces(1, 3)
+        for lo in (0, 256):
+            for m in range(M_TILES):
+                pass_g(1, 3, m, lo, lo + 128)
+                pass_g(1, 3, m, lo + 128, lo + 256)
+                pass_u(1, 3, m, lo, lo + 256)
         for m in range(M_TILES):
             silu(1, m)
             mul(1, m)
+            store(1, m)

@@ -19,6 +19,7 @@ P = 128
 PASSES = K // 512
 HALF = 512
 M_TILES = M // 128
+WARM = 3
 V_COLS = 352
 
 
@@ -33,17 +34,16 @@ def tile_mix_glu48_fm_none_kernel(tc, x, w4_words, w4_scales, w8_words, w8_scale
         sc8 = keep.tile([P, M], U8, align_bytes=64, name="sc8")
         dummy = keep.tile([P, 8], F32, align_bytes=64, name="dummy")
         nc.vector.memset(sc8[:].bitcast(I32), 0)
-        nc.gpsimd.memset(sc4[:].bitcast(I32), 0)
+        nc.vector.memset(sc4[:].bitcast(I32), 0)
         nc.vector.memset(dummy[:], 0.0)
-        nc.scalar.activation(out=dummy[:, 0:1], in_=dummy[:, 1:2], func=ACT.Silu)
 
         raw = {}
         w4 = {}
         w8 = {}
 
-        def load_x(h, a, pieces=1):
+        def load_x(h, a, pieces=1, which=(0, 1)):
             width = HALF // pieces
-            for c in range(pieces):
+            for c in which[:pieces]:
                 t = keep.tile([P, 4, width], F32, align_bytes=64, name="raw_%d_%d_%d" % (h, a, c))
                 for lo in range(0, width, 256):
                     raw[h, a, width * c + lo] = t[:, :, lo : lo + 256]
@@ -54,30 +54,46 @@ def tile_mix_glu48_fm_none_kernel(tc, x, w4_words, w4_scales, w8_words, w8_scale
                     ),
                 )
 
-        def load_w(a):
+        def load_w8(a):
             w8[a] = keep.tile([P, 4 * M], U8, align_bytes=64, name="w8_%d" % a)
-            w4[a] = keep.tile([P, 2 * M], U8, align_bytes=64, name="w4_%d" % a)
             nc.sync.dma_start(out=w8[a][:].bitcast(I32), in_=w8_words[a].rearrange("p n i -> p (n i)").bitcast(I32))
-            nc.sync.dma_start(out=w4[a][:].bitcast(I32), in_=w4_words[a].bitcast(I32))
 
-        def load_scales():
+        def load_w4(a, n):
+            t = keep.tile([P, n, 2 * M], U8, align_bytes=64, name="w4_%d" % a)
+            for i in range(n):
+                w4[a + i] = t[:, i, :]
+            nc.sync.dma_start(
+                out=t[:].bitcast(I32), in_=w4_words[a : a + n].rearrange("a p b -> p a b").bitcast(I32)
+            )
+
+        def load_sc8():
             for q in range(4):
                 nc.scalar.dma_start(
                     out=sc8[32 * q : 32 * q + 16, :].bitcast(I32),
                     in_=w8_scales[:, 4 * q : 4 * q + 4, :].bitcast(I32),
                 )
+
+        def load_sc4():
             for q in range(4):
-                nc.gpsimd.dma_start(
+                nc.scalar.dma_start(
                     out=sc4[32 * q : 32 * q + 4, :].bitcast(I32).rearrange("r (a n) -> r a n", a=PASSES),
                     in_=w4_scales[:, 4 * q : 4 * q + 4, :].bitcast(I32).rearrange("a r n -> r a n"),
                 )
 
-        load_scales()
-        load_x(0, 0, 2)
-        load_w(0)
-        for a in range(1, PASSES):
-            load_x(0, a)
-            load_w(a)
+        load_sc8()
+        nc.scalar.activation(out=dummy[:, 0:1], in_=dummy[:, 1:2], func=ACT.Silu)
+        load_x(0, 0, 2, (0,))
+        load_w8(0)
+        load_x(0, 0, 2, (1,))
+        load_w4(0, 1)
+        load_x(0, 1)
+        load_sc4()
+        load_w8(1)
+        load_w4(1, 3)
+        load_x(0, 2)
+        load_w8(2)
+        load_x(0, 3)
+        load_w8(3)
         for a in range(PASSES - 1):
             load_x(1, a)
         load_x(1, PASSES - 1, 2)
@@ -146,13 +162,21 @@ def tile_mix_glu48_fm_none_kernel(tc, x, w4_words, w4_scales, w8_words, w8_scale
 
         gate = {}
         res = {}
+        pair = {}
 
         def open_banks(h):
             for m in range(M_TILES):
                 g[h, m] = psum.tile([P, HALF], F32, name="g_%d_%d" % (h, m), tag="g_%d" % m)
                 u[h, m] = psum.tile([P, HALF], F32, name="u_%d_%d" % (h, m), tag="u_%d" % m)
                 gate[h, m] = keep.tile([P, HALF], F32, align_bytes=64, name="gate_%d_%d" % (h, m))
-                res[h, m] = keep.tile([P, HALF], F32, align_bytes=64, name="res_%d_%d" % (h, m))
+                if h == 1:
+                    res[h, m] = keep.tile([P, HALF], F32, align_bytes=64, name="res_%d_%d" % (h, m))
+            if h == 0:
+                for m in (0, 2):
+                    t = keep.tile([P, 2, HALF], F32, align_bytes=64, name="res_%d_%d" % (h, m))
+                    pair[m] = t
+                    res[h, m] = t[:, 0, :]
+                    res[h, m + 1] = t[:, 1, :]
 
         def silu(h, m, lo=0, hi=HALF):
             nc.scalar.activation(out=gate[h, m][:, lo:hi], in_=g[h, m][:, lo:hi], func=ACT.Silu)
@@ -162,9 +186,9 @@ def tile_mix_glu48_fm_none_kernel(tc, x, w4_words, w4_scales, w8_words, w8_scale
                 out=res[h, m][:, lo:hi], in0=u[h, m][:, lo:hi], in1=gate[h, m][:, lo:hi], op=ALU.mult
             )
 
-        def store(h, m):
+        def store(h, m, lo=0, hi=HALF):
             nc.sync.dma_start(
-                out=out[128 * m : 128 * (m + 1), HALF * h : HALF * (h + 1)], in_=res[h, m][:]
+                out=out[128 * m : 128 * (m + 1), HALF * h + lo : HALF * h + hi], in_=res[h, m][:, lo:hi]
             )
 
         def multiply(h, a):
@@ -172,7 +196,29 @@ def tile_mix_glu48_fm_none_kernel(tc, x, w4_words, w4_scales, w8_words, w8_scale
                 pass_g(h, a, m, 0, HALF)
                 pass_u(h, a, m, 0, HALF)
 
+        def multiply_u_first(h, a):
+            for m in range(M_TILES):
+                pass_u(h, a, m, 0, HALF)
+            for m in range(M_TILES):
+                pass_g(h, a, m, 0, HALF)
+
+        def multiply_g_first(h, a):
+            for m in range(M_TILES):
+                pass_g(h, a, m, 0, HALF)
+            for m in range(M_TILES):
+                pass_u(h, a, m, 0, HALF)
+
         open_banks(0)
+        for m in range(WARM):
+            nc.tensor.matmul_mx(
+                out=g[0, m][:],
+                lhsT=w8[0][:, 0:512].bitcast(FP8X4),
+                lhsT_scale=sc8[:, 0:128],
+                rhs=w8[0][:].bitcast(FP8X4),
+                rhs_scale=sc8[:],
+                start=True,
+                stop=True,
+            )
         prepare_pieces(0, 0)
         for m in range(M_TILES):
             pass_u(0, 0, m, 0, HALF)
@@ -182,7 +228,10 @@ def tile_mix_glu48_fm_none_kernel(tc, x, w4_words, w4_scales, w8_words, w8_scale
             copies_whole(0, a)
             quantize(0, a, 0)
             quantize(0, a, 256)
-            multiply(0, a)
+            if a == 1 or a == 3:
+                multiply_u_first(0, a) if a == 1 else multiply_g_first(0, a)
+            else:
+                multiply(0, a)
 
         open_banks(1)
         silu(0, 0)
@@ -195,8 +244,10 @@ def tile_mix_glu48_fm_none_kernel(tc, x, w4_words, w4_scales, w8_words, w8_scale
         silu(0, 3)
         for m in (1, 2, 3):
             mul(0, m)
-        for m in range(M_TILES):
-            store(0, m)
+        for m in (0, 2):
+            nc.sync.dma_start(
+                out=out[128 * m : 128 * (m + 2), 0:HALF].rearrange("(m p) w -> p m w", p=P), in_=pair[m][:]
+            )
         multiply(1, 0)
         for a in (1, 2):
             copies_whole(1, a)
@@ -204,12 +255,12 @@ def tile_mix_glu48_fm_none_kernel(tc, x, w4_words, w4_scales, w8_words, w8_scale
             quantize(1, a, 256)
             multiply(1, a)
         prepare_pieces(1, 3)
-        for lo in (0, 256):
-            for m in range(M_TILES):
-                pass_g(1, 3, m, lo, lo + 128)
-                pass_g(1, 3, m, lo + 128, lo + 256)
-                pass_u(1, 3, m, lo, lo + 256)
-        for m in range(M_TILES):
+        multiply(1, 3)
+        for m in range(M_TILES - 1):
             silu(1, m)
             mul(1, m)
             store(1, m)
+        silu(1, 3)
+        for lo in (0, 256):
+            mul(1, 3, lo, lo + 256)
+            store(1, 3, lo, lo + 256)

@@ -19,8 +19,7 @@ P = 128
 PASSES = K // 512
 HALF = 512
 M_TILES = M // 128
-WARM = 3
-V_COLS = 352
+V_COLS = 320
 
 
 def tile_mix_glu48_fm_none_kernel(tc, x, w4_words, w4_scales, w8_words, w8_scales, out):
@@ -82,21 +81,20 @@ def tile_mix_glu48_fm_none_kernel(tc, x, w4_words, w4_scales, w8_words, w8_scale
 
         load_sc8()
         nc.scalar.activation(out=dummy[:, 0:1], in_=dummy[:, 1:2], func=ACT.Silu)
-        load_x(0, 0, 2, (0,))
-        load_w8(0)
-        load_x(0, 0, 2, (1,))
+        load_x(0, 0, 2)
         load_w4(0, 1)
+        load_w8(0)
         load_x(0, 1)
         load_sc4()
-        load_w8(1)
         load_w4(1, 3)
+        load_w8(1)
         load_x(0, 2)
-        load_w8(2)
         load_x(0, 3)
+        load_w8(2)
+        load_x(1, 0, 2)
         load_w8(3)
-        for a in range(PASSES - 1):
-            load_x(1, a)
-        load_x(1, PASSES - 1, 2)
+        for a in range(1, PASSES):
+            load_x(1, a, 2)
 
         grouped = {}
         codes = {}
@@ -127,12 +125,17 @@ def tile_mix_glu48_fm_none_kernel(tc, x, w4_words, w4_scales, w8_words, w8_scale
             interleave(nc.vector.tensor_copy, h, a, 256, V_COLS)
             interleave(nc.scalar.copy, h, a, V_COLS, HALF)
 
+        def copy_piece_v(h, a, lo):
+            interleave(nc.vector.tensor_copy, h, a, lo, lo + V_COLS // 2)
+
+        def copy_piece_s(h, a, lo):
+            interleave(nc.scalar.copy, h, a, lo + V_COLS // 2, lo + 256)
+
         def prepare_pieces(h, a):
             tiles(h, a)
             for lo in (0, 256):
-                interleave(nc.vector.tensor_copy, h, a, lo, lo + 128)
-                interleave(nc.vector.tensor_copy, h, a, lo + 128, lo + 160)
-                interleave(nc.scalar.copy, h, a, lo + 160, lo + 256)
+                copy_piece_v(h, a, lo)
+                copy_piece_s(h, a, lo)
                 quantize(h, a, lo)
 
         g = {}
@@ -208,59 +211,62 @@ def tile_mix_glu48_fm_none_kernel(tc, x, w4_words, w4_scales, w8_words, w8_scale
             for m in range(M_TILES):
                 pass_u(h, a, m, 0, HALF)
 
+        def multiply_g_first(h, a):
+            for m in range(M_TILES):
+                pass_g(h, a, m, 0, HALF)
+            for m in range(M_TILES):
+                pass_u(h, a, m, 0, HALF)
+
         open_banks(0)
-        for m in range(WARM):
-            nc.tensor.matmul_mx(
-                out=g[0, m][:],
-                lhsT=w8[0][:, 0:512].bitcast(FP8X4),
-                lhsT_scale=sc8[:, 0:128],
-                rhs=w8[0][:].bitcast(FP8X4),
-                rhs_scale=sc8[:],
-                start=True,
-                stop=True,
-            )
         prepare_pieces(0, 0)
-        for m in range(M_TILES):
-            pass_u(0, 0, m, 0, HALF)
-        for m in range(M_TILES):
-            pass_g(0, 0, m, 0, HALF)
+        multiply_u_first(0, 0)
         for a in range(1, PASSES):
             copies_whole(0, a)
             quantize(0, a, 0)
             quantize(0, a, 256)
-            if a == 1 or a == 3:
-                multiply_u_first(0, a) if a == 1 else multiply_g_first(0, a)
+            if a == 1:
+                multiply_u_first(0, a)
             else:
-                multiply(0, a)
+                multiply_g_first(0, a)
 
         open_banks(1)
+        prepare_pieces(1, 0)
+        tiles(1, 1)
         silu(0, 0)
-        silu(0, 1)
-        copies_whole(1, 0)
         mul(0, 0)
-        quantize(1, 0, 0)
-        quantize(1, 0, 256)
+        silu(0, 1)
+        mul(0, 1)
         silu(0, 2)
         silu(0, 3)
-        for m in (1, 2, 3):
-            mul(0, m)
+        copy_piece_v(1, 1, 0)
+        copy_piece_s(1, 1, 0)
+        mul(0, 2)
+        quantize(1, 1, 0)
+        copy_piece_v(1, 1, 256)
+        copy_piece_s(1, 1, 256)
+        mul(0, 3)
+        quantize(1, 1, 256)
+        multiply(1, 0)
+        multiply(1, 1)
+        prepare_pieces(1, 2)
+        multiply(1, 2)
+        prepare_pieces(1, 3)
+        for m in (0, 1):
+            pass_g(1, 3, m, 0, HALF)
+            pass_u(1, 3, m, 0, HALF)
+        for m in (2, 3):
+            pass_g(1, 3, m, 0, HALF)
+        for m in (2, 3):
+            pass_u(1, 3, m, 0, HALF)
         for m in (0, 2):
             nc.sync.dma_start(
                 out=out[128 * m : 128 * (m + 2), 0:HALF].rearrange("(m p) w -> p m w", p=P), in_=pair[m][:]
             )
-        multiply(1, 0)
-        for a in (1, 2):
-            copies_whole(1, a)
-            quantize(1, a, 0)
-            quantize(1, a, 256)
-            multiply(1, a)
-        prepare_pieces(1, 3)
-        multiply(1, 3)
         for m in range(M_TILES - 1):
             silu(1, m)
             mul(1, m)
             store(1, m)
-        silu(1, 3)
         for lo in (0, 256):
+            silu(1, 3, lo, lo + 256)
             mul(1, 3, lo, lo + 256)
             store(1, 3, lo, lo + 256)

from contextlib import ExitStack

import concourse.mybir as mybir

K, M, T = 2048, 512, 1024
FLOPS = 2 * 2 * K * M * T

F32 = mybir.dt.float32
BF16 = mybir.dt.bfloat16
I32 = mybir.dt.int32
U32 = mybir.dt.uint32
U8 = mybir.dt.uint8
FP8X4 = mybir.dt.float8_e4m3fn_x4
FP4X4 = mybir.dt.float4_e2m1fn_x4
ACT = mybir.ActivationFunctionType
ALU = mybir.AluOpType

P = 128
PASSES = K // 512
HALF = 512
M_TILES = M // 128
V_COLS = 320


def tile_mix_glu48_fm_none_kernel(tc, x, w4_words, w4_scales, w8_words, w8_scales, out):
    nc = tc.nc
    with ExitStack() as ctx:
        keep = ctx.enter_context(tc.tile_pool(name="keep", bufs=1))
        psum = ctx.enter_context(tc.psum_pool(name="psum", bufs=1))
        ctx.enter_context(tc.manual_schedule())

        sc4 = keep.tile([P, PASSES * M], U8, align_bytes=64, name="sc4")
        sc8 = keep.tile([P, M], U8, align_bytes=64, name="sc8")
        dummy = keep.tile([P, 8], F32, align_bytes=64, name="dummy")
        nc.vector.memset(sc8[:].bitcast(I32), 0)
        nc.vector.memset(sc4[:].bitcast(I32), 0)
        nc.vector.memset(dummy[:], 0.0)

        raw = {}
        w4 = {}
        w8 = {}

        def load_x(h, a, pieces=1, which=(0, 1)):
            width = HALF // pieces
            for c in which[:pieces]:
                t = keep.tile([P, 4, width], F32, align_bytes=64, name="raw_%d_%d_%d" % (h, a, c))
                for lo in range(0, width, 256):
                    raw[h, a, width * c + lo] = t[:, :, lo : lo + 256]
                nc.sync.dma_start(
                    out=t[:],
                    in_=x[512 * a : 512 * (a + 1), HALF * h + width * c : HALF * h + width * (c + 1)].rearrange(
                        "(p j) w -> p j w", j=4
                    ),
                )

        def load_w8(a):
            w8[a] = keep.tile([P, 4 * M], U8, align_bytes=64, name="w8_%d" % a)
            nc.sync.dma_start(out=w8[a][:].bitcast(I32), in_=w8_words[a].rearrange("p n i -> p (n i)").bitcast(I32))

        def load_w4(a, n):
            t = keep.tile([P, n, 2 * M], U8, align_bytes=64, name="w4_%d" % a)
            for i in range(n):
                w4[a + i] = t[:, i, :]
            nc.sync.dma_start(
                out=t[:].bitcast(I32), in_=w4_words[a : a + n].rearrange("a p b -> p a b").bitcast(I32)
            )

        def load_sc8():
            for q in range(4):
                nc.scalar.dma_start(
                    out=sc8[32 * q : 32 * q + 16, :].bitcast(I32),
                    in_=w8_scales[:, 4 * q : 4 * q + 4, :].bitcast(I32),
                )

        def load_sc4():
            for q in range(4):
                nc.scalar.dma_start(
                    out=sc4[32 * q : 32 * q + 4, :].bitcast(I32).rearrange("r (a n) -> r a n", a=PASSES),
                    in_=w4_scales[:, 4 * q : 4 * q + 4, :].bitcast(I32).rearrange("a r n -> r a n"),
                )

        load_sc8()
        nc.scalar.activation(out=dummy[:, 0:1], in_=dummy[:, 1:2], func=ACT.Silu)
        load_x(0, 0, 2)
        load_w4(0, 1)
        load_w8(0)
        load_x(0, 1)
        load_sc4()
        load_w4(1, 3)
        load_w8(1)
        load_x(0, 2)
        load_x(0, 3)
        load_w8(2)
        load_x(1, 0, 2)
        load_w8(3)
        for a in range(1, PASSES):
            load_x(1, a, 2)

        grouped = {}
        codes = {}
        scales = {}

        def interleave(engine_copy, h, a, lo, hi):
            base = lo // 256 * 256
            engine_copy(
                out=grouped[h, a][:, lo:hi, :].rearrange("p (c i) t -> p c t i", i=4),
                in_=raw[h, a, base][:, :, lo - base : hi - base].rearrange("p t (c i) -> p c t i", i=4),
            )

        def tiles(h, a):
            grouped[h, a] = keep.tile([P, HALF, 4], BF16, align_bytes=64, name="grouped_%d_%d" % (h, a))
            codes[h, a] = keep.tile([P, HALF], U32, align_bytes=64, name="codes_%d_%d" % (h, a))
            scales[h, a] = keep.tile([P, HALF], U8, align_bytes=64, name="scales_%d_%d" % (h, a))

        def quantize(h, a, lo):
            nc.vector.quantize_mx(
                out=codes[h, a][:, lo : lo + 256].bitcast(FP8X4),
                scales=scales[h, a][:, lo : lo + 256],
                in_=grouped[h, a][:, lo : lo + 256, :].rearrange("p w t -> p (w t)"),
            )

        def copies_whole(h, a):
            tiles(h, a)
            interleave(nc.vector.tensor_copy, h, a, 0, 256)
            interleave(nc.vector.tensor_copy, h, a, 256, V_COLS)
            interleave(nc.scalar.copy, h, a, V_COLS, HALF)

        def copy_piece_v(h, a, lo):
            interleave(nc.vector.tensor_copy, h, a, lo, lo + V_COLS // 2)

        def copy_piece_s(h, a, lo):
            interleave(nc.scalar.copy, h, a, lo + V_COLS // 2, lo + 256)

        def prepare_pieces(h, a):
            tiles(h, a)
            for lo in (0, 256):
                copy_piece_v(h, a, lo)
                copy_piece_s(h, a, lo)
                quantize(h, a, lo)

        g = {}
        u = {}

        def pass_g(h, a, m, lo, hi):
            nc.tensor.matmul_mx(
                out=g[h, m][:, lo:hi],
                lhsT=w4[a][:, 256 * m : 256 * (m + 1)].bitcast(FP4X4),
                lhsT_scale=sc4[:, M * a + 128 * m : M * a + 128 * (m + 1)],
                rhs=codes[h, a][:, lo:hi].bitcast(FP8X4),
                rhs_scale=scales[h, a][:, lo:hi],
                start=(a == 0),
                stop=(a == PASSES - 1 and hi == HALF),
            )

        def pass_u(h, a, m, lo, hi):
            nc.tensor.matmul_mx(
                out=u[h, m][:, lo:hi],
                lhsT=w8[a][:, 512 * m : 512 * (m + 1)].bitcast(FP8X4),
                lhsT_scale=sc8[4 * a : P, 128 * m : 128 * (m + 1)],
                rhs=codes[h, a][:, lo:hi].bitcast(FP8X4),
                rhs_scale=scales[h, a][:, lo:hi],
                start=(a == 0),
                stop=(a == PASSES - 1 and hi == HALF),
            )

        gate = {}
        res = {}
        pair = {}

        def open_banks(h):
            for m in range(M_TILES):
                g[h, m] = psum.tile([P, HALF], F32, name="g_%d_%d" % (h, m), tag="g_%d" % m)
                u[h, m] = psum.tile([P, HALF], F32, name="u_%d_%d" % (h, m), tag="u_%d" % m)
                gate[h, m] = keep.tile([P, HALF], F32, align_bytes=64, name="gate_%d_%d" % (h, m))
                if h == 1:
                    res[h, m] = keep.tile([P, HALF], F32, align_bytes=64, name="res_%d_%d" % (h, m))
            if h == 0:
                for m in (0, 2):
                    t = keep.tile([P, 2, HALF], F32, align_bytes=64, name="res_%d_%d" % (h, m))
                    pair[m] = t
                    res[h, m] = t[:, 0, :]
                    res[h, m + 1] = t[:, 1, :]

        def silu(h, m, lo=0, hi=HALF):
            nc.scalar.activation(out=gate[h, m][:, lo:hi], in_=g[h, m][:, lo:hi], func=ACT.Silu)

        def mul(h, m, lo=0, hi=HALF):
            nc.vector.tensor_tensor(
                out=res[h, m][:, lo:hi], in0=u[h, m][:, lo:hi], in1=gate[h, m][:, lo:hi], op=ALU.mult
            )

        def store(h, m, lo=0, hi=HALF):
            nc.sync.dma_start(
                out=out[128 * m : 128 * (m + 1), HALF * h + lo : HALF * h + hi], in_=res[h, m][:, lo:hi]
            )

        def multiply(h, a):
            for m in range(M_TILES):
                pass_g(h, a, m, 0, HALF)
                pass_u(h, a, m, 0, HALF)

        def multiply_u_first(h, a):
            for m in range(M_TILES):
                pass_u(h, a, m, 0, HALF)
            for m in range(M_TILES):
                pass_g(h, a, m, 0, HALF)

        def multiply_g_first(h, a):
            for m in range(M_TILES):
                pass_g(h, a, m, 0, HALF)
            for m in range(M_TILES):
                pass_u(h, a, m, 0, HALF)

        def multiply_g_first(h, a):
            for m in range(M_TILES):
                pass_g(h, a, m, 0, HALF)
            for m in range(M_TILES):
                pass_u(h, a, m, 0, HALF)

        open_banks(0)
        prepare_pieces(0, 0)
        multiply_u_first(0, 0)
        for a in range(1, PASSES):
            copies_whole(0, a)
            quantize(0, a, 0)
            quantize(0, a, 256)
            if a == 1:
                multiply_u_first(0, a)
            else:
                multiply_g_first(0, a)

        open_banks(1)
        prepare_pieces(1, 0)
        tiles(1, 1)
        silu(0, 0)
        mul(0, 0)
        silu(0, 1)
        mul(0, 1)
        silu(0, 2)
        silu(0, 3)
        copy_piece_v(1, 1, 0)
        copy_piece_s(1, 1, 0)
        mul(0, 2)
        quantize(1, 1, 0)
        copy_piece_v(1, 1, 256)
        copy_piece_s(1, 1, 256)
        mul(0, 3)
        quantize(1, 1, 256)
        multiply(1, 0)
        multiply(1, 1)
        prepare_pieces(1, 2)
        multiply(1, 2)
        prepare_pieces(1, 3)
        for m in (0, 1):
            pass_g(1, 3, m, 0, HALF)
            pass_u(1, 3, m, 0, HALF)
        for m in (2, 3):
            pass_g(1, 3, m, 0, HALF)
        for m in (2, 3):
            pass_u(1, 3, m, 0, HALF)
        for m in (0, 2):
            nc.sync.dma_start(
                out=out[128 * m : 128 * (m + 2), 0:HALF].rearrange("(m p) w -> p m w", p=P), in_=pair[m][:]
            )
        for m in range(M_TILES - 1):
            silu(1, m)
            mul(1, m)
            store(1, m)
        for lo in (0, 256):
            silu(1, 3, lo, lo + 256)
            mul(1, 3, lo, lo + 256)
            store(1, 3, lo, lo + 256)
